import numpy as np, ml_dtypes
CORES = [113,118,241,246]
N = 4
import mx_ref
NC, ROOT = 128, 1
C = np.float32(0.029)
BF = ml_dtypes.bfloat16
def cut(t, i, w=512):
    return t[:, w * i:w * i + w]
def tile(rs):
    return np.stack(rs, axis=2).reshape(128, -1).astype(BF)
def pick(b):
    s = np.zeros((128, 128, 4), np.float32)
    s[np.arange(128), np.arange(128), b] = 1.0
    return mx_ref.quantize(s.reshape(128, 512).astype(BF))
def pk(c, s, i=0):
    return (np.ascontiguousarray(c[:, 512 * i:512 * i + 512]), mx_ref.live(s[:, 128 * i:128 * i + 128]))
def inputs(rng, e, E):
    def f(*shape):
        v = (rng.standard_normal(shape, dtype=np.float32) * np.exp2(rng.integers(-2, 3, shape[:-1] + (1,)))).astype(BF)
        return mx_ref.spread((v.astype(np.float32) * np.exp2(rng.integers(-E, E + 1, shape[:-2] + (1, 1))).astype(np.float32)).astype(BF), rng, e)
    def packed(k):
        c = np.zeros((N, 128, k * 512), np.uint8); s = np.zeros((N, 128, k * 128), np.uint8)
        for r in range(N):
            for i in range(k):
                a, b = mx_ref.quantize(f(128, 512)); c[r][:, 512 * i:512 * i + 512] = a; s[r][:, 128 * i:128 * i + 128] = mx_ref.plane(b, rng)
        return c, s
    d = {}
    d["wc"], d["ws"] = packed(1)
    d["a"] = f(N, 128, 512)
    d["bb"] = f(N, 128, 4 * 512)
    d["x"] = f(N, 128, 4 * NC)
    return d
def setup_inputs(rng):
    return inputs(rng, 0, 0)
def setup_inputs_blocks(rng):
    return inputs(rng, 2, 0)
def setup_inputs_wide(rng):
    return inputs(rng, 0, 3)
def reference(wc, ws, a, bb, x):
    S = [pick(t) for t in range(4)]; A = mx_ref.quantize(a[ROOT])
    V = [mx_ref.quantize(tile([mx_ref.matmul(S[t], pk(wc[j], ws[j])) + mx_ref.matmul(mx_ref.quantize(cut(bb[j], t)), A) * C for t in range(4)])) for j in range(N)]
    y = np.zeros((N, 128, N * NC), np.float32)
    for r in range(N):
        X = mx_ref.quantize(x[r])
        for j in range(N):
            y[r][:, NC * j:NC * j + NC] = mx_ref.matmul(V[j], X)
    return {"y": y}

@@ -1,0 +1,165 @@
+from concourse.bass import DstId, RemoteDMATransfer
+from concourse.mybir import dt, AluOpType, ActivationFunctionType
+
+NB = 128
+SCRATCH = {
+    "e": ("sbuf", [128, 516], "bfloat16"),
+    "sq": ("sbuf", [128, 512], "float8_e4m3fn_x4"), "ss": ("sbuf", [128, 512], "uint8"),
+    "wq": ("sbuf", [128, 128], "float8_e4m3fn_x4"), "wsc": ("sbuf", [128, 128], "uint8"),
+    "at": ("sbuf", [128, 512], "bfloat16"),
+    "aq": ("sbuf", [128, 128], "float8_e4m3fn_x4"), "asc": ("sbuf", [128, 128], "uint8"),
+    "bt": ("sbuf", [128, 2048], "bfloat16"),
+    "bq": ("sbuf", [128, 512], "float8_e4m3fn_x4"), "bsc": ("sbuf", [128, 512], "uint8"),
+    "xt": ("sbuf", [128, 512], "bfloat16"),
+    "xq": ("sbuf", [128, 128], "float8_e4m3fn_x4"), "xsc": ("sbuf", [128, 128], "uint8"),
+    "t": ("sbuf", [128, 512], "float32"),
+    "v": ("sbuf", [128, 512], "bfloat16"),
+    "vq": ("sbuf", [128, 512], "float8_e4m3fn_x4"), "vsc": ("sbuf", [128, 512], "uint8"),
+    "yo": ("sbuf", [128, 512], "float32"),
+    "dp": ("psum", [128, 2048], "float32"),
+    "pp": ("psum", [128, 2048], "float32"),
+}
+SEMAPHORES = ["lda", "ldw", "ldb", "ldx", "go", "ez", "es", "sqd", "bqd", "xqd", "aqd", "ain", "asent", "d",
+              "p0", "p1", "p2", "p3", "t0", "t1", "t2", "t3", "ad", "vqd", "vin0", "vin1", "vin2", "vin3", "vsent",
+              "y0", "y1", "y2", "y3", "e0", "e1", "st0", "st1"]
+C = 0.029
+
+
+def cols(j):
+    return slice(NB * j, NB * j + NB)
+
+
+def split(src, T, topo):
+    others = [c for c in T.cores if c != src]
+    near = [c for c in others if topo.host(c) == topo.host(src) and topo.chip(c) == topo.chip(src)]
+    far = [c for c in others if c not in near]
+    fm = topo.mask(src, far[0])
+    for c in far:
+        fm &= topo.mask(src, c)
+    nm = topo.mask(src, near[0]) & ~fm
+    bits = [k for k in range(nm.bit_length()) if nm >> k & 1][::2]
+    return [(far, fm), (near, sum(1 << k for k in bits))]
+
+
+def engines(src, dst, T, topo):
+    for group, m in split(src, T, topo):
+        if dst in group:
+            return bin(m).count("1")
+
+
+def send(g, core, T, topo, ap, remote_sem, local_sem):
+    transfers, n = [], 0
+    for group, m in split(core, T, topo):
+        ids = []
+        for c in group:
+            rid, pid = topo.addr(c, core)
+            ids.append(DstId(rid=rid, pnc=pid))
+        transfers.append(RemoteDMATransfer(dst_ids=ids, dma_engine_mask=m, remote_sem=remote_sem, srcs=[ap], dsts=[ap] * len(ids)))
+        n += bin(m).count("1")
+    g.remote_dma_fused(transfers, local_sem=local_sem)
+    return n
+
+
+def rank_program(g, core, T, topo):
+    rank = T.rank_of(core)
+    if rank is None:
+        return
+    s = T.sem
+    n_ranks = len(T.cores)
+    root = T.root
+    is_root = rank == root
+    order = [rank] + [j for j in [root] + [k for k in range(n_ranks) if k != root] if j != rank]
+    order = [j for i, j in enumerate(order) if j not in order[:i]]
+    u8 = dt.uint8
+    per_call = sum(bin(m).count("1") for _, m in split(core, T, topo))
+
+    if is_root:
+        g.sync.dma_start(T.at[:], T.a[:]).then_inc(s.lda, 16)
+        g.sync.sem_inc(s.go, 1)
+        g.scalar.wait_ge(s.go, 1)
+    g.scalar.dma_start(T.bt[:], T.bb[:]).then_inc(s.ldb, 16)
+    g.sync.dma_start(T.wq[:].bitcast(u8), T.wc[:]).then_inc(s.ldw, 16)
+    g.sync.dma_start(T.wsc[:], T.ws[:]).then_inc(s.ldw, 16)
+    if is_root:
+        g.sync.wait_ge(s.asent, 2 * per_call)
+    g.sync.dma_start(T.xt[:], T.x[:]).then_inc(s.ldx, 16)
+
+    g.vector.memset(T.e[:], 0.0).then_inc(s.ez, 1)
+    g.wait_ge(s.ez, 1)
+    g.affine_select(out=T.e[:, 3:512:4], in_=T.e[:, 3:512:4], pattern=[[-1, 128]], compare_op=AluOpType.not_equal, fill=1.0,
+                    base=0, channel_multiplier=1).then_inc(s.es, 1)
+
+    if is_root:
+        g.vector.wait_ge(s.lda, 16)
+        g.vector.quantize_mx(T.aq[:], T.asc[:], T.at[:]).then_inc(s.aqd, 1)
+    g.vector.wait_ge(s.es, 1)
+    for b in range(4):
+        g.vector.quantize_mx(T.sq[:, cols(b)], T.ss[:, cols(b)], T.e[:, 3 - b:515 - b]).then_inc(s.sqd, 1)
+    g.vector.wait_ge(s.ldb, 16)
+    g.vector.quantize_mx(T.bq[:], T.bsc[:], T.bt[:]).then_inc(s.bqd, 1)
+    if not is_root:
+        g.vector.wait_ge(s.ldx, 16)
+        g.vector.quantize_mx(T.xq[:], T.xsc[:], T.xt[:]).then_inc(s.xqd, 1)
+
+    if is_root:
+        g.wait_ge(s.aqd, 1)
+        send(g, core, T, topo, T.aq[:].bitcast(u8), s.ain, s.asent)
+        send(g, core, T, topo, T.asc[:], s.ain, s.asent)
+
+    g.tensor.wait_ge(s.ldw, 32)
+    g.tensor.wait_ge(s.sqd, 4)
+    for b in range(4):
+        g.tensor.matmul_mx(T.dp[:, 512 * b:512 * b + NB], T.sq[:, cols(b)], T.ss[:, cols(b)], T.wq[:], T.wsc[:],
+                           True, True).then_inc(s.d, 1)
+    g.tensor.wait_ge(s.bqd, 1)
+    if is_root:
+        g.tensor.wait_ge(s.aqd, 1)
+    else:
+        g.tensor.wait_ge(s.ain, 2 * engines(T.cores[root], core, T, topo))
+    for b in range(4):
+        g.tensor.matmul_mx(T.pp[:, 512 * b:512 * b + NB], T.bq[:, cols(b)], T.bsc[:, cols(b)], T.aq[:], T.asc[:],
+                           True, True).then_inc(s["p%d" % b], 1)
+
+    for b in range(4):
+        g.scalar.wait_ge(s["p%d" % b], 1)
+        g.scalar.activation(T.t[:, cols(b)], T.pp[:, 512 * b:512 * b + NB], ActivationFunctionType.Copy,
+                            scale=C).then_inc(s["t%d" % b], 1)
+    g.vector.wait_ge(s.d, 4)
+    for b in range(4):
+        g.vector.wait_ge(s["t%d" % b], 1)
+        g.vector.tensor_tensor(T.v[:, b:512:4], T.dp[:, 512 * b:512 * b + NB], T.t[:, cols(b)], AluOpType.add).then_inc(s.ad, 1)
+    g.vector.wait_ge(s.ad, 4)
+    own = (T.vq[:, cols(rank)], T.vsc[:, cols(rank)])
+    g.vector.quantize_mx(own[0], own[1], T.v[:]).then_inc(s.vqd, 1)
+    if is_root:
+        g.vector.wait_ge(s.ldx, 16)
+        g.vector.quantize_mx(T.xq[:], T.xsc[:], T.xt[:]).then_inc(s.xqd, 1)
+
+    g.wait_ge(s.vqd, 1)
+    vin = s["vin%d" % rank]
+    send(g, core, T, topo, own[0].bitcast(u8), vin, s.vsent)
+    send(g, core, T, topo, own[1], vin, s.vsent)
+
+    g.tensor.wait_ge(s.xqd, 1)
+    for j in order:
+        if j == rank:
+            g.tensor.wait_ge(s.vqd, 1)
+        else:
+            g.tensor.wait_ge(s["vin%d" % j], 2 * engines(T.cores[j], core, T, topo))
+        g.tensor.matmul_mx(T.pp[:, 512 * j:512 * j + NB], T.vq[:, cols(j)], T.vsc[:, cols(j)], T.xq[:], T.xsc[:],
+                           True, True).then_inc(s["y%d" % j], 1)
+    for j in order:
+        out, in_, done = T.yo[:, cols(j)], T.pp[:, 512 * j:512 * j + NB], s["e%d" % (j // 2)]
+        if j % 2 == 0:
+            g.vector.wait_ge(s["y%d" % j], 1)
+            g.vector.tensor_copy(out, in_).then_inc(done, 1)
+        else:
+            g.scalar.wait_ge(s["y%d" % j], 1)
+            g.scalar.activation(out, in_, ActivationFunctionType.Copy).then_inc(done, 1)
+    g.sync.wait_ge(s.vsent, 2 * per_call)
+    g.sync.wait_ge(s.e0, 2)
+    g.sync.dma_start(T.y[:, 0:2 * NB], T.yo[:, 0:2 * NB]).then_inc(s.st0, 16)
+    g.scalar.wait_ge(s.e1, 2)
+    g.scalar.dma_start(T.y[:, 2 * NB:4 * NB], T.yo[:, 2 * NB:4 * NB]).then_inc(s.st1, 16)
+    g.sync.wait_ge(s.st0, 16)
+    g.scalar.wait_ge(s.st1, 16)

@@ -19,14 +19,23 @@ SCRATCH = {
     "dp": ("psum", [128, 2048], "float32"),
     "pp": ("psum", [128, 2048], "float32"),
 }
-SEMAPHORES = ["lda", "ldw", "ldb", "ldx", "go", "ez", "es", "sqd", "bqd", "xqd", "aqd", "ain", "asent", "d",
-              "p0", "p1", "p2", "p3", "t0", "t1", "t2", "t3", "ad", "vqd", "vin0", "vin1", "vin2", "vin3", "vsent",
-              "y0", "y1", "y2", "y3", "e0", "e1", "st0", "st1"]
+SEMAPHORES = ["lda", "ldw", "ldb0", "ldb1", "ldx", "go", "ez", "es", "sqd", "bqd0", "bqd1", "xqd", "aqd", "ain", "asent", "d",
+              "p0", "p1", "p2", "p3", "t0", "t1", "t2", "t3", "ad", "vqd", "vin0", "vin1", "vin2", "vin3", "first", "rest",
+              "vsent", "y0", "y1", "y2", "y3", "e0", "e1", "e2", "e3", "st0", "st1"]
 C = 0.029
 
 
 def cols(j):
     return slice(NB * j, NB * j + NB)
+
+
+def count(mask):
+    return bin(mask).count("1")
+
+
+def halves(mask):
+    bits = [1 << k for k in range(mask.bit_length()) if mask >> k & 1]
+    return sum(bits[:len(bits) // 2]), sum(bits[len(bits) // 2:])
 
 
 def split(src, T, topo):
@@ -44,20 +53,63 @@ def split(src, T, topo):
 def engines(src, dst, T, topo):
     for group, m in split(src, T, topo):
         if dst in group:
-            return bin(m).count("1")
+            return count(m)
+
+
+def transfer(core, dsts, ap, mask, sem, topo):
+    ids = []
+    for c in dsts:
+        rid, pid = topo.addr(c, core)
+        ids.append(DstId(rid=rid, pnc=pid))
+    return RemoteDMATransfer(dst_ids=ids, dma_engine_mask=mask, remote_sem=sem, srcs=[ap], dsts=[ap] * len(ids))
 
 
 def send(g, core, T, topo, ap, remote_sem, local_sem):
-    transfers, n = [], 0
-    for group, m in split(core, T, topo):
-        ids = []
-        for c in group:
-            rid, pid = topo.addr(c, core)
-            ids.append(DstId(rid=rid, pnc=pid))
-        transfers.append(RemoteDMATransfer(dst_ids=ids, dma_engine_mask=m, remote_sem=remote_sem, srcs=[ap], dsts=[ap] * len(ids)))
-        n += bin(m).count("1")
-    g.remote_dma_fused(transfers, local_sem=local_sem)
+    parts = split(core, T, topo)
+    g.remote_dma_fused([transfer(core, group, ap, m, remote_sem, topo) for group, m in parts], local_sem=local_sem)
+    return sum(count(m) for _, m in parts)
+
+
+def root_calls(T, topo):
+    root = T.cores[T.root]
+    (far, fm), (near, nm) = split(root, T, topo)
+    near, (fa, fb) = near[0], far
+    via = [c for c in far if topo.die(c) == topo.die(near)][0]
+    other = [c for c in far if c != via][0]
+    f0, f1 = halves(fm)
+    n0, n1 = halves(nm)
+    q = NB // 4
+
+    def out(c):
+        return split(c, T, topo)[0][1]
+
+    return [(root, [([fa], "q", 0, q, f0, "first"), ([fb], "q", q, 2 * q, f1, "first"), ([near], "s", 0, NB, nm, "first")]),
+            (root, [(far, "q", 2 * q, NB, fm, "rest"), ([near], "q", 0, 2 * q, n0, "rest"),
+                    ([near], "q", 2 * q, NB, n1, "rest")]),
+            (root, [([other], "s", 0, NB, fm, "rest")]),
+            (near, [([via], "s", 0, NB, out(near), "rest")]),
+            (fa, [([fb], "q", 0, q, out(fa), "rest")]),
+            (fb, [([fa], "q", q, 2 * q, out(fb), "rest")])]
+
+
+def send_root_part(g, core, T, topo):
+    n, base = 0, NB * T.root
+    for src, parts in root_calls(T, topo):
+        if src == core:
+            transfers = []
+            for dsts, kind, lo, hi, m, sem in parts:
+                if kind == "q":
+                    ap = T.vq[:, base + lo:base + hi].bitcast(dt.uint8)
+                else:
+                    ap = T.vsc[:, base + lo:base + hi]
+                transfers.append(transfer(core, dsts, ap, m, T.sem[sem], topo))
+                n += count(m)
+            g.remote_dma_fused(transfers, local_sem=T.sem.vsent)
     return n
+
+
+def root_arrivals(core, T, topo, sem):
+    return sum(count(p[4]) for _, parts in root_calls(T, topo) for p in parts if p[5] == sem and core in p[0])
 
 
 def rank_program(g, core, T, topo):
@@ -71,18 +123,19 @@ def rank_program(g, core, T, topo):
     order = [rank] + [j for j in [root] + [k for k in range(n_ranks) if k != root] if j != rank]
     order = [j for i, j in enumerate(order) if j not in order[:i]]
     u8 = dt.uint8
-    per_call = sum(bin(m).count("1") for _, m in split(core, T, topo))
+    per_call = sum(count(m) for _, m in split(core, T, topo))
 
     if is_root:
         g.sync.dma_start(T.at[:], T.a[:]).then_inc(s.lda, 16)
         g.sync.sem_inc(s.go, 1)
         g.scalar.wait_ge(s.go, 1)
-    g.scalar.dma_start(T.bt[:], T.bb[:]).then_inc(s.ldb, 16)
+    for h in range(2):
+        w = slice(1024 * h, 1024 * h + 1024)
+        g.scalar.dma_start(T.bt[:, w], T.bb[:, w]).then_inc(s["ldb%d" % h], 16)
     g.sync.dma_start(T.wq[:].bitcast(u8), T.wc[:]).then_inc(s.ldw, 16)
     g.sync.dma_start(T.wsc[:], T.ws[:]).then_inc(s.ldw, 16)
-    if is_root:
-        g.sync.wait_ge(s.asent, 2 * per_call)
-    g.sync.dma_start(T.xt[:], T.x[:]).then_inc(s.ldx, 16)
+    if not is_root:
+        g.sync.dma_start(T.xt[:], T.x[:]).then_inc(s.ldx, 16)
 
     g.vector.memset(T.e[:], 0.0).then_inc(s.ez, 1)
     g.wait_ge(s.ez, 1)
@@ -95,8 +148,10 @@ def rank_program(g, core, T, topo):
     g.vector.wait_ge(s.es, 1)
     for b in range(4):
         g.vector.quantize_mx(T.sq[:, cols(b)], T.ss[:, cols(b)], T.e[:, 3 - b:515 - b]).then_inc(s.sqd, 1)
-    g.vector.wait_ge(s.ldb, 16)
-    g.vector.quantize_mx(T.bq[:], T.bsc[:], T.bt[:]).then_inc(s.bqd, 1)
+    for h in range(2):
+        w = slice(2 * NB * h, 2 * NB * h + 2 * NB)
+        g.vector.wait_ge(s["ldb%d" % h], 16)
+        g.vector.quantize_mx(T.bq[:, w], T.bsc[:, w], T.bt[:, 1024 * h:1024 * h + 1024]).then_inc(s["bqd%d" % h], 1)
     if not is_root:
         g.vector.wait_ge(s.ldx, 16)
         g.vector.quantize_mx(T.xq[:], T.xsc[:], T.xt[:]).then_inc(s.xqd, 1)
@@ -111,12 +166,15 @@ def rank_program(g, core, T, topo):
     for b in range(4):
         g.tensor.matmul_mx(T.dp[:, 512 * b:512 * b + NB], T.sq[:, cols(b)], T.ss[:, cols(b)], T.wq[:], T.wsc[:],
                            True, True).then_inc(s.d, 1)
-    g.tensor.wait_ge(s.bqd, 1)
     if is_root:
         g.tensor.wait_ge(s.aqd, 1)
     else:
+        g.tensor.wait_ge(s.bqd0, 1)
+        g.tensor.wait_ge(s.bqd1, 1)
         g.tensor.wait_ge(s.ain, 2 * engines(T.cores[root], core, T, topo))
     for b in range(4):
+        if is_root and b % 2 == 0:
+            g.tensor.wait_ge(s["bqd%d" % (b // 2)], 1)
         g.tensor.matmul_mx(T.pp[:, 512 * b:512 * b + NB], T.bq[:, cols(b)], T.bsc[:, cols(b)], T.aq[:], T.asc[:],
                            True, True).then_inc(s["p%d" % b], 1)
 
@@ -135,31 +193,43 @@ def rank_program(g, core, T, topo):
         g.vector.wait_ge(s.ldx, 16)
         g.vector.quantize_mx(T.xq[:], T.xsc[:], T.xt[:]).then_inc(s.xqd, 1)
 
-    g.wait_ge(s.vqd, 1)
-    vin = s["vin%d" % rank]
-    send(g, core, T, topo, own[0].bitcast(u8), vin, s.vsent)
-    send(g, core, T, topo, own[1], vin, s.vsent)
+    if is_root:
+        g.wait_ge(s.vqd, 1)
+        left = send_root_part(g, core, T, topo)
+        g.sync.wait_ge(s.asent, 2 * per_call)
+        g.sync.wait_ge(s.vsent, left)
+        g.sync.dma_start(T.xt[:], T.x[:]).then_inc(s.ldx, 16)
+    else:
+        g.wait_ge(s.first, root_arrivals(core, T, topo, "first"))
+        left = send_root_part(g, core, T, topo)
+        g.wait_ge(s.vqd, 1)
+        vin = s["vin%d" % rank]
+        left += send(g, core, T, topo, own[0].bitcast(u8), vin, s.vsent)
+        left += send(g, core, T, topo, own[1], vin, s.vsent)
+        g.sync.wait_ge(s.vsent, left)
 
     g.tensor.wait_ge(s.xqd, 1)
     for j in order:
         if j == rank:
             g.tensor.wait_ge(s.vqd, 1)
+        elif j == root:
+            g.tensor.wait_ge(s.first, root_arrivals(core, T, topo, "first"))
+            g.tensor.wait_ge(s.rest, root_arrivals(core, T, topo, "rest"))
         else:
             g.tensor.wait_ge(s["vin%d" % j], 2 * engines(T.cores[j], core, T, topo))
         g.tensor.matmul_mx(T.pp[:, 512 * j:512 * j + NB], T.vq[:, cols(j)], T.vsc[:, cols(j)], T.xq[:], T.xsc[:],
                            True, True).then_inc(s["y%d" % j], 1)
-    for j in order:
-        out, in_, done = T.yo[:, cols(j)], T.pp[:, 512 * j:512 * j + NB], s["e%d" % (j // 2)]
-        if j % 2 == 0:
+    for i, j in enumerate(order):
+        out, in_, done = T.yo[:, cols(j)], T.pp[:, 512 * j:512 * j + NB], s["e%d" % i]
+        if i % 2 == 0:
             g.vector.wait_ge(s["y%d" % j], 1)
             g.vector.tensor_copy(out, in_).then_inc(done, 1)
         else:
             g.scalar.wait_ge(s["y%d" % j], 1)
             g.scalar.activation(out, in_, ActivationFunctionType.Copy).then_inc(done, 1)
-    g.sync.wait_ge(s.vsent, 2 * per_call)
-    g.sync.wait_ge(s.e0, 2)
-    g.sync.dma_start(T.y[:, 0:2 * NB], T.yo[:, 0:2 * NB]).then_inc(s.st0, 16)
-    g.scalar.wait_ge(s.e1, 2)
-    g.scalar.dma_start(T.y[:, 2 * NB:4 * NB], T.yo[:, 2 * NB:4 * NB]).then_inc(s.st1, 16)
-    g.sync.wait_ge(s.st0, 16)
+    for i, j in enumerate(order):
+        q, st = (g.scalar, s.st1) if i == n_ranks - 1 else (g.sync, s.st0)
+        q.wait_ge(s["e%d" % i], 1)
+        q.dma_start(T.y[:, cols(j)], T.yo[:, cols(j)]).then_inc(st, 16)
+    g.sync.wait_ge(s.st0, 16 * (n_ranks - 1))
     g.scalar.wait_ge(s.st1, 16)

from concourse.bass import DstId, RemoteDMATransfer
from concourse.mybir import dt, AluOpType, ActivationFunctionType

NB = 128
SCRATCH = {
    "e": ("sbuf", [128, 516], "bfloat16"),
    "sq": ("sbuf", [128, 512], "float8_e4m3fn_x4"), "ss": ("sbuf", [128, 512], "uint8"),
    "wq": ("sbuf", [128, 128], "float8_e4m3fn_x4"), "wsc": ("sbuf", [128, 128], "uint8"),
    "at": ("sbuf", [128, 512], "bfloat16"),
    "aq": ("sbuf", [128, 128], "float8_e4m3fn_x4"), "asc": ("sbuf", [128, 128], "uint8"),
    "bt": ("sbuf", [128, 2048], "bfloat16"),
    "bq": ("sbuf", [128, 512], "float8_e4m3fn_x4"), "bsc": ("sbuf", [128, 512], "uint8"),
    "xt": ("sbuf", [128, 512], "bfloat16"),
    "xq": ("sbuf", [128, 128], "float8_e4m3fn_x4"), "xsc": ("sbuf", [128, 128], "uint8"),
    "t": ("sbuf", [128, 512], "float32"),
    "v": ("sbuf", [128, 512], "bfloat16"),
    "vq": ("sbuf", [128, 512], "float8_e4m3fn_x4"), "vsc": ("sbuf", [128, 512], "uint8"),
    "yo": ("sbuf", [128, 512], "float32"),
    "dp": ("psum", [128, 2048], "float32"),
    "pp": ("psum", [128, 2048], "float32"),
}
SEMAPHORES = ["lda", "ldw", "ldb0", "ldb1", "ldx", "go", "ez", "es", "sqd", "bqd0", "bqd1", "xqd", "aqd", "ain", "asent", "d",
              "p0", "p1", "p2", "p3", "t0", "t1", "t2", "t3", "ad", "vqd", "vin0", "vin1", "vin2", "vin3", "first", "rest",
              "vsent", "y0", "y1", "y2", "y3", "e0", "e1", "e2", "e3", "st0", "st1"]
C = 0.029


def cols(j):
    return slice(NB * j, NB * j + NB)


def count(mask):
    return bin(mask).count("1")


def halves(mask):
    bits = [1 << k for k in range(mask.bit_length()) if mask >> k & 1]
    return sum(bits[:len(bits) // 2]), sum(bits[len(bits) // 2:])


def split(src, T, topo):
    others = [c for c in T.cores if c != src]
    near = [c for c in others if topo.host(c) == topo.host(src) and topo.chip(c) == topo.chip(src)]
    far = [c for c in others if c not in near]
    fm = topo.mask(src, far[0])
    for c in far:
        fm &= topo.mask(src, c)
    nm = topo.mask(src, near[0]) & ~fm
    bits = [k for k in range(nm.bit_length()) if nm >> k & 1][::2]
    return [(far, fm), (near, sum(1 << k for k in bits))]


def engines(src, dst, T, topo):
    for group, m in split(src, T, topo):
        if dst in group:
            return count(m)


def transfer(core, dsts, ap, mask, sem, topo):
    ids = []
    for c in dsts:
        rid, pid = topo.addr(c, core)
        ids.append(DstId(rid=rid, pnc=pid))
    return RemoteDMATransfer(dst_ids=ids, dma_engine_mask=mask, remote_sem=sem, srcs=[ap], dsts=[ap] * len(ids))


def send(g, core, T, topo, ap, remote_sem, local_sem):
    parts = split(core, T, topo)
    g.remote_dma_fused([transfer(core, group, ap, m, remote_sem, topo) for group, m in parts], local_sem=local_sem)
    return sum(count(m) for _, m in parts)


def root_calls(T, topo):
    root = T.cores[T.root]
    (far, fm), (near, nm) = split(root, T, topo)
    near, (fa, fb) = near[0], far
    via = [c for c in far if topo.die(c) == topo.die(near)][0]
    other = [c for c in far if c != via][0]
    f0, f1 = halves(fm)
    n0, n1 = halves(nm)
    q = NB // 4

    def out(c):
        return split(c, T, topo)[0][1]

    return [(root, [([fa], "q", 0, q, f0, "first"), ([fb], "q", q, 2 * q, f1, "first"), ([near], "s", 0, NB, nm, "first")]),
            (root, [(far, "q", 2 * q, NB, fm, "rest"), ([near], "q", 0, 2 * q, n0, "rest"),
                    ([near], "q", 2 * q, NB, n1, "rest")]),
            (root, [([other], "s", 0, NB, fm, "rest")]),
            (near, [([via], "s", 0, NB, out(near), "rest")]),
            (fa, [([fb], "q", 0, q, out(fa), "rest")]),
            (fb, [([fa], "q", q, 2 * q, out(fb), "rest")])]


def send_root_part(g, core, T, topo):
    n, base = 0, NB * T.root
    for src, parts in root_calls(T, topo):
        if src == core:
            transfers = []
            for dsts, kind, lo, hi, m, sem in parts:
                if kind == "q":
                    ap = T.vq[:, base + lo:base + hi].bitcast(dt.uint8)
                else:
                    ap = T.vsc[:, base + lo:base + hi]
                transfers.append(transfer(core, dsts, ap, m, T.sem[sem], topo))
                n += count(m)
            g.remote_dma_fused(transfers, local_sem=T.sem.vsent)
    return n


def root_arrivals(core, T, topo, sem):
    return sum(count(p[4]) for _, parts in root_calls(T, topo) for p in parts if p[5] == sem and core in p[0])


def rank_program(g, core, T, topo):
    rank = T.rank_of(core)
    if rank is None:
        return
    s = T.sem
    n_ranks = len(T.cores)
    root = T.root
    is_root = rank == root
    order = [rank] + [j for j in [root] + [k for k in range(n_ranks) if k != root] if j != rank]
    order = [j for i, j in enumerate(order) if j not in order[:i]]
    u8 = dt.uint8
    per_call = sum(count(m) for _, m in split(core, T, topo))

    if is_root:
        g.sync.dma_start(T.at[:], T.a[:]).then_inc(s.lda, 16)
        g.sync.sem_inc(s.go, 1)
        g.scalar.wait_ge(s.go, 1)
    for h in range(2):
        w = slice(1024 * h, 1024 * h + 1024)
        g.scalar.dma_start(T.bt[:, w], T.bb[:, w]).then_inc(s["ldb%d" % h], 16)
    g.sync.dma_start(T.wq[:].bitcast(u8), T.wc[:]).then_inc(s.ldw, 16)
    g.sync.dma_start(T.wsc[:], T.ws[:]).then_inc(s.ldw, 16)
    if not is_root:
        g.sync.dma_start(T.xt[:], T.x[:]).then_inc(s.ldx, 16)

    g.vector.memset(T.e[:], 0.0).then_inc(s.ez, 1)
    g.wait_ge(s.ez, 1)
    g.affine_select(out=T.e[:, 3:512:4], in_=T.e[:, 3:512:4], pattern=[[-1, 128]], compare_op=AluOpType.not_equal, fill=1.0,
                    base=0, channel_multiplier=1).then_inc(s.es, 1)

    if is_root:
        g.vector.wait_ge(s.lda, 16)
        g.vector.quantize_mx(T.aq[:], T.asc[:], T.at[:]).then_inc(s.aqd, 1)
    g.vector.wait_ge(s.es, 1)
    for b in range(4):
        g.vector.quantize_mx(T.sq[:, cols(b)], T.ss[:, cols(b)], T.e[:, 3 - b:515 - b]).then_inc(s.sqd, 1)
    for h in range(2):
        w = slice(2 * NB * h, 2 * NB * h + 2 * NB)
        g.vector.wait_ge(s["ldb%d" % h], 16)
        g.vector.quantize_mx(T.bq[:, w], T.bsc[:, w], T.bt[:, 1024 * h:1024 * h + 1024]).then_inc(s["bqd%d" % h], 1)
    if not is_root:
        g.vector.wait_ge(s.ldx, 16)
        g.vector.quantize_mx(T.xq[:], T.xsc[:], T.xt[:]).then_inc(s.xqd, 1)

    if is_root:
        g.wait_ge(s.aqd, 1)
        send(g, core, T, topo, T.aq[:].bitcast(u8), s.ain, s.asent)
        send(g, core, T, topo, T.asc[:], s.ain, s.asent)

    g.tensor.wait_ge(s.ldw, 32)
    g.tensor.wait_ge(s.sqd, 4)
    for b in range(4):
        g.tensor.matmul_mx(T.dp[:, 512 * b:512 * b + NB], T.sq[:, cols(b)], T.ss[:, cols(b)], T.wq[:], T.wsc[:],
                           True, True).then_inc(s.d, 1)
    if is_root:
        g.tensor.wait_ge(s.aqd, 1)
    else:
        g.tensor.wait_ge(s.bqd0, 1)
        g.tensor.wait_ge(s.bqd1, 1)
        g.tensor.wait_ge(s.ain, 2 * engines(T.cores[root], core, T, topo))
    for b in range(4):
        if is_root and b % 2 == 0:
            g.tensor.wait_ge(s["bqd%d" % (b // 2)], 1)
        g.tensor.matmul_mx(T.pp[:, 512 * b:512 * b + NB], T.bq[:, cols(b)], T.bsc[:, cols(b)], T.aq[:], T.asc[:],
                           True, True).then_inc(s["p%d" % b], 1)

    for b in range(4):
        g.scalar.wait_ge(s["p%d" % b], 1)
        g.scalar.activation(T.t[:, cols(b)], T.pp[:, 512 * b:512 * b + NB], ActivationFunctionType.Copy,
                            scale=C).then_inc(s["t%d" % b], 1)
    g.vector.wait_ge(s.d, 4)
    for b in range(4):
        g.vector.wait_ge(s["t%d" % b], 1)
        g.vector.tensor_tensor(T.v[:, b:512:4], T.dp[:, 512 * b:512 * b + NB], T.t[:, cols(b)], AluOpType.add).then_inc(s.ad, 1)
    g.vector.wait_ge(s.ad, 4)
    own = (T.vq[:, cols(rank)], T.vsc[:, cols(rank)])
    g.vector.quantize_mx(own[0], own[1], T.v[:]).then_inc(s.vqd, 1)
    if is_root:
        g.vector.wait_ge(s.ldx, 16)
        g.vector.quantize_mx(T.xq[:], T.xsc[:], T.xt[:]).then_inc(s.xqd, 1)

    if is_root:
        g.wait_ge(s.vqd, 1)
        left = send_root_part(g, core, T, topo)
        g.sync.wait_ge(s.asent, 2 * per_call)
        g.sync.wait_ge(s.vsent, left)
        g.sync.dma_start(T.xt[:], T.x[:]).then_inc(s.ldx, 16)
    else:
        g.wait_ge(s.first, root_arrivals(core, T, topo, "first"))
        left = send_root_part(g, core, T, topo)
        g.wait_ge(s.vqd, 1)
        vin = s["vin%d" % rank]
        left += send(g, core, T, topo, own[0].bitcast(u8), vin, s.vsent)
        left += send(g, core, T, topo, own[1], vin, s.vsent)
        g.sync.wait_ge(s.vsent, left)

    g.tensor.wait_ge(s.xqd, 1)
    for j in order:
        if j == rank:
            g.tensor.wait_ge(s.vqd, 1)
        elif j == root:
            g.tensor.wait_ge(s.first, root_arrivals(core, T, topo, "first"))
            g.tensor.wait_ge(s.rest, root_arrivals(core, T, topo, "rest"))
        else:
            g.tensor.wait_ge(s["vin%d" % j], 2 * engines(T.cores[j], core, T, topo))
        g.tensor.matmul_mx(T.pp[:, 512 * j:512 * j + NB], T.vq[:, cols(j)], T.vsc[:, cols(j)], T.xq[:], T.xsc[:],
                           True, True).then_inc(s["y%d" % j], 1)
    for i, j in enumerate(order):
        out, in_, done = T.yo[:, cols(j)], T.pp[:, 512 * j:512 * j + NB], s["e%d" % i]
        if i % 2 == 0:
            g.vector.wait_ge(s["y%d" % j], 1)
            g.vector.tensor_copy(out, in_).then_inc(done, 1)
        else:
            g.scalar.wait_ge(s["y%d" % j], 1)
            g.scalar.activation(out, in_, ActivationFunctionType.Copy).then_inc(done, 1)
    for i, j in enumerate(order):
        q, st = (g.scalar, s.st1) if i == n_ranks - 1 else (g.sync, s.st0)
        q.wait_ge(s["e%d" % i], 1)
        q.dma_start(T.y[:, cols(j)], T.yo[:, cols(j)]).then_inc(st, 16)
    g.sync.wait_ge(s.st0, 16 * (n_ranks - 1))
    g.scalar.wait_ge(s.st1, 16)
